import numpy as np, ml_dtypes
CORES = [17,57,65,89,97,121]
N = 6
TK, NT = 256, 3
def setup_inputs(rng):
    x = rng.standard_normal((NT, 128, TK), dtype=np.float32).astype(ml_dtypes.bfloat16)
    return {"x": np.broadcast_to(x, (2, NT, 128, TK)).reshape(N, 128, TK).copy(), "w": rng.standard_normal((N, 128, NT * 128), dtype=np.float32).astype(ml_dtypes.bfloat16)}
def setup_inputs_big(rng):
    d = setup_inputs(rng)
    for k in ("x", "w"): d[k] = (d[k].astype(np.float32) * 1024.0).astype(d[k].dtype)
    return d
def setup_inputs_small(rng):
    d = setup_inputs(rng)
    for k in ("x", "w"): d[k] = (d[k].astype(np.float32) * (1 / 1024.0)).astype(d[k].dtype)
    return d
def setup_inputs_apart(rng):
    d = setup_inputs(rng)
    f = (10.0 ** rng.permutation(np.linspace(-1.5, 1.5, N))).astype(np.float32).reshape(N, 1, 1)
    for k in ("x", "w"): d[k] = (d[k].astype(np.float32) * f).astype(d[k].dtype)
    return d
def tie_inputs(x):
    x = dict(x)
    x["x"] = np.concatenate([x["x"][:NT], x["x"][:NT]])
    return x
def reference(x, w):
    X, W = x.astype(np.float64), w.astype(np.float64)
    y = np.stack([sum(W[r][:, 128 * j:128 * j + 128].T @ X[j if r < NT else j + NT] for j in range(NT)) for r in range(N)])
    return {"y": y.astype(ml_dtypes.bfloat16 if x.dtype != np.float64 else np.float64)}

from concourse.bass import DstId, RemoteDMATransfer

NT = 3
TK = 256
P = 128

SCRATCH = {
    "xt0": ("sbuf", [P, TK], "bfloat16"),
    "xt1": ("sbuf", [P, TK], "bfloat16"),
    "xt2": ("sbuf", [P, TK], "bfloat16"),
    "ws": ("sbuf", [P, NT * P], "bfloat16"),
    "acc": ("psum", [P, TK], "float32"),
    "ys": ("sbuf", [P, TK], "bfloat16"),
}
SEMAPHORES = ["xl", "wl", "arr0", "arr1", "arr2", "sent", "mm", "cp", "st"]


def _distance(topo, src, dst):
    if not topo.may_write(src, dst):
        return None
    a, b = topo.chip(src), topo.chip(dst)
    if a == b:
        return 0
    if topo.same_plane(a, b) or topo.mates(a, b):
        return 1
    return 2


def _source(topo, cores, dst, j):
    holders = [c for i, c in enumerate(cores) if i % NT == j]
    if dst in holders:
        return dst
    ranked = [(_distance(topo, c, dst), c) for c in holders]
    return min((d, c) for d, c in ranked if d is not None)[1]


def rank_program(g, core, T, topo):
    rank = T.rank_of(core)
    if rank is None:
        return
    cores = list(T.cores)
    mine = rank % NT
    slot = [T["xt%d" % j] for j in range(NT)]
    arr = [T.sem["arr%d" % j] for j in range(NT)]

    takers = [c for c in cores if c != core and _source(topo, cores, c, mine) == core]
    takers.sort(key=lambda c: (T.rank_of(c) % NT - mine) % NT)

    common = topo.mask(core, takers[0])
    for c in takers[1:]:
        common &= topo.mask(core, c)
    engines = [e for e in range(16) if (common >> e) & 1]
    n_eng = 1
    while n_eng * 2 <= len(engines):
        n_eng *= 2
    send_mask = sum(1 << e for e in engines[:n_eng])

    g.sync.dma_start(slot[mine][:], T.x[:]).then_inc(T.sem.xl, 16)
    g.sync.dma_start(T.ws[:], T.w[:]).then_inc(T.sem.wl, 16)

    g.wait_ge(T.sem.xl, 16)
    ids = []
    for c in takers:
        rid, pid, _ = topo.addr(c)
        ids.append(DstId(rid=rid, pnc=pid))
    g.remote_dma_fused(
        [RemoteDMATransfer(dst_ids=ids, dma_engine_mask=send_mask, remote_sem=arr[mine],
                           srcs=[slot[mine][:]], dsts=[slot[mine][:] for _ in takers])],
        local_sem=T.sem.sent)
    g.wait_ge(T.sem.sent, n_eng)

    order = [mine] + [(mine - k) % NT for k in range(1, NT)]
    g.tensor.wait_ge(T.sem.xl, 16)
    g.tensor.wait_ge(T.sem.wl, 16)
    for k, j in enumerate(order):
        if j != mine:
            g.tensor.wait_ge(arr[j], n_eng)
        mmv = g.tensor.matmul(T.acc[:], T.ws[:, P * j:P * (j + 1)], slot[j][:], k == 0, k == NT - 1)
    mmv.then_inc(T.sem.mm, 1)

    g.vector.wait_ge(T.sem.mm, 1)
    g.vector.tensor_copy(T.ys[:], T.acc[:]).then_inc(T.sem.cp, 1)

    g.sync.wait_ge(T.sem.cp, 1)
    g.sync.dma_start(T.y[:], T.ys[:]).then_inc(T.sem.st, 16)
    g.sync.wait_ge(T.sem.st, 16)
